import numpy as np
import ml_dtypes


def mxq(x, axis, fmt="e4m3"):
    dtype, down = {"e4m3": (ml_dtypes.float8_e4m3fn, 7), "e5m2": (ml_dtypes.float8_e5m2, 14)}[fmt]
    v = np.moveaxis(np.asarray(x, np.float32).astype(ml_dtypes.bfloat16).astype(np.float64), axis, -1)
    blocks = v.reshape(v.shape[:-1] + (-1, 32))
    amax = np.abs(blocks).max(-1, keepdims=True)
    byte = np.maximum(np.where(amax > 0, np.frexp(amax)[1] - 1 + 127, 0) - down, 1)
    scale = np.exp2(byte - 127.0)
    codes = (blocks / scale).astype(np.float32).astype(dtype).astype(np.float64)
    return np.moveaxis((codes * scale).reshape(v.shape), -1, axis)


WIDE = False


def mx_kscale(k):
    if not WIDE:
        return np.ones(k)
    levels = np.array([10, -10, 5, -5, 0])
    if k % 512:
        return np.exp2(np.random.permutation(np.resize(levels, k // 32))).repeat(32)
    a = np.empty((k // 512, 16))
    for p in range(k // 512):
        a[p, :8] = np.random.permutation(np.resize(levels, 8))
        for g in range(8):
            far = levels[np.abs(levels - a[p, g]) >= 10]
            a[p, g + 8] = far[np.random.randint(len(far))]
    return np.exp2(a.ravel()).repeat(32)


def f64(x):
    return np.asarray(x).astype(np.float64)


def striped(idx):
    return np.tile(idx.reshape(-1, 16).T, (8, 1)).astype(np.uint16)


def unstriped(offs):
    return offs[:16].T.reshape(-1).astype(np.int64)


def striped8(idx):
    return np.concatenate([x.reshape(-1, 16).T for x in idx]).astype(np.uint16)


def runs(offs, k):
    lists = np.stack([offs[16 * r : 16 * r + 16].T.reshape(-1) for r in range(8)]).astype(np.int64)
    return lists[np.arange(k) % 512 // 64]


def pack_weight(w):
    k, n = w.shape
    w = f64(np.asarray(w, np.float32).astype(ml_dtypes.bfloat16)).reshape(k // 32, 32, n)
    amax = np.abs(w).max(1)
    byte = np.clip(np.where(amax > 0, np.frexp(amax)[1] - 1 + 127 - 7, 1), 1, 254)
    scaled = (w * np.exp2(127.0 - byte)[:, None, :]).reshape(k, n).astype(np.float32)
    words = np.ascontiguousarray(scaled.reshape(k // 512, 128, 4, n).transpose(0, 1, 3, 2)).astype(ml_dtypes.float8_e4m3fn).view(np.uint8)
    return words, np.ascontiguousarray(byte.astype(np.uint8).reshape(k // 512, 16, n))


def unpack_weight(words, scales):
    g, p, n, _ = words.shape
    vals = np.ascontiguousarray(words).view(ml_dtypes.float8_e4m3fn).astype(np.float64) * np.repeat(np.exp2(scales.astype(np.float64) - 127.0), 8, axis=1)[..., None]
    return vals.transpose(0, 1, 3, 2).reshape(g * 512, n)


def sigmoid(v):
    return 1.0 / (1.0 + np.exp(-np.maximum(v, -700.0)))

def planes(y):
    n, m = y.shape
    v = y.astype(np.float32).astype(ml_dtypes.bfloat16).astype(np.float64).reshape(n // 32, 32, m)
    top = np.abs(v).max(1)
    byte = np.clip(np.where(top > 0, np.frexp(top)[1] - 1 + 127 - 7, 1), 1, 254)
    codes = (v * np.exp2(127.0 - byte)[:, None, :]).reshape(n, m).astype(np.float32).astype(ml_dtypes.float8_e4m3fn).view(np.uint8)
    words = codes.reshape(n // 512, 128, 4, m).transpose(0, 1, 3, 2)
    return np.ascontiguousarray(words), np.ascontiguousarray(byte.astype(np.uint8).reshape(n // 512, 16, m))


K, T, S, N, H = 512, 2048, 512, 512, 512


def setup_inputs():
    n = np.random.standard_normal
    s = mx_kscale(K)[:, None]
    u = mx_kscale(H)
    packed_xT = pack_weight(n((K, T)) * s)
    packed_w1 = pack_weight(n((K, H)) / np.sqrt(K) / s)
    packed_w2 = pack_weight(n((H, N)) / np.sqrt(H) / u[:, None])
    return {
        "x_words": packed_xT[0],
        "x_scales": packed_xT[1],
        "w1_words": packed_w1[0],
        "w1_scales": packed_w1[1],
        "gn": (np.random.uniform(0.5, 1.5, (H, 1)) * u[:, None]).astype(np.float32),
        "w2_words": packed_w2[0],
        "w2_scales": packed_w2[1],
        "offs": striped(np.random.permutation(T)[:S]),
        "n1": striped8(np.stack([np.random.permutation(S) for _ in range(8)])),
        "n2": striped8(np.stack([np.random.permutation(S) for _ in range(8)])),
        "n3": striped8(np.stack([np.random.permutation(S) for _ in range(8)])),
        "n4": striped8(np.stack([np.random.permutation(S) for _ in range(8)])),
    }


def reference(x_words, x_scales, w1_words, w1_scales, gn, w2_words, w2_scales, offs, n1, n2, n3, n4):
    xq = unpack_weight(x_words, x_scales)[:, unstriped(offs)]
    y = unpack_weight(w1_words, w1_scales).T @ xq
    st = y[np.arange(H)[:, None], runs(n1, H)] - y
    z = f64(gn) * (y * (sigmoid(st[np.arange(H)[:, None], runs(n2, H)])))
    h = unpack_weight(w2_words, w2_scales).T @ mxq(z, 0, "e4m3")
    out_0 = h - (np.minimum(h[np.arange(N)[:, None], runs(n3, N)], h[np.arange(N)[:, None], runs(n4, N)]))
    return (out_0,) + planes(out_0)

@@ -1,0 +1,201 @@
+from contextlib import ExitStack
+
+import concourse.mybir as mybir
+
+K, T, S, N, H = 512, 2048, 512, 512, 512
+FLOPS = 2 * K * H * S + 2 * H * N * S
+
+F32 = mybir.dt.float32
+BF16 = mybir.dt.bfloat16
+I32 = mybir.dt.int32
+U32 = mybir.dt.uint32
+U16 = mybir.dt.uint16
+U8 = mybir.dt.uint8
+FP8X4 = mybir.dt.float8_e4m3fn_x4
+ALU = mybir.AluOpType
+ACT = mybir.ActivationFunctionType
+
+P = 128
+PACK = 4
+LIST_ROWS = 16
+W2_ROW = 4
+HALVES = [(0, 256), (256, 512)]
+CHUNKS = [(0, 256), (256, 384), (384, 512)]
+
+
+def as_words(dram):
+    return dram[0].rearrange("p n t -> p (n t)").bitcast(I32)
+
+
+def entries(lst, lo, hi):
+    return lst[:, lo // LIST_ROWS : hi // LIST_ROWS]
+
+
+def load_scale_rows(queue, plane, first_row, dram):
+    for q in range(4):
+        queue.dma_start(
+            out=plane[32 * q + first_row : 32 * q + first_row + 4, :].bitcast(I32),
+            in_=dram[0][4 * q : 4 * q + 4, :].bitcast(I32),
+        )
+
+
+def by_pairs(planes):
+    return planes.rearrange("p t (c i) -> p c t i", i=2)
+
+
+def woven(tile):
+    return tile.rearrange("p (c i t) -> p c t i", i=2, t=PACK)
+
+
+def tile_picked_layhopdunder_none_po_kernel(
+    tc, x_words, x_scales, w1_words, w1_scales, gn, w2_words, w2_scales, offs, n1, n2, n3, n4, out_0, out_1, out_2
+):
+    nc = tc.nc
+    with ExitStack() as ctx:
+        lists = ctx.enter_context(tc.tile_pool(name="lists", bufs=1))
+        sb = ctx.enter_context(tc.tile_pool(name="sb", bufs=1))
+        ps = ctx.enter_context(tc.psum_pool(name="ps", bufs=1))
+
+        x_scale_table = sb.tile([P, T], U8, align_bytes=64)
+        w1_scale_raw = sb.tile([P, H], U8, align_bytes=64)
+        w2_scale_raw = sb.tile([P, N], U8, align_bytes=64)
+        y_window = [sb.tile([P, 2 * S], F32, name="y_window%d" % t) for t in range(PACK)]
+        warm = sb.tile([P, 1], F32)
+        warm_out = sb.tile([P, 1], F32)
+        nc.gpsimd.memset(warm[:], 0.0)
+        nc.vector.memset(x_scale_table[:].bitcast(I32), 0)
+        for t in range(PACK):
+            nc.vector.memset(y_window[t][:, S:], 0.0)
+        nc.vector.memset(w1_scale_raw[:].bitcast(I32), 0)
+        nc.vector.memset(w2_scale_raw[:].bitcast(I32), 0)
+
+        offs_sb = lists.tile([P, S // LIST_ROWS], U16)
+        n1_sb = lists.tile([P, S // LIST_ROWS], U16)
+        n2_sb = lists.tile([P, S // LIST_ROWS], U16)
+        n3_sb = lists.tile([P, S // LIST_ROWS], U16)
+        n4_sb = lists.tile([P, S // LIST_ROWS], U16)
+        x_word_table = sb.tile([P, T], U32, align_bytes=64)
+        w1_raw = sb.tile([P, H], I32, align_bytes=64, tag="w_raw")
+        gain = sb.tile([P, PACK], F32)
+
+        nc.sync.dma_start(offs_sb[:], offs)
+        nc.scalar.dma_start(out=w1_raw[:], in_=as_words(w1_words))
+        nc.scalar.dma_start(out=x_word_table[:].bitcast(I32), in_=as_words(x_words))
+        load_scale_rows(nc.sync, x_scale_table, 0, x_scales)
+        nc.scalar.activation(warm_out[:], warm[:], ACT.Sigmoid)
+        load_scale_rows(nc.scalar, w1_scale_raw, 0, w1_scales)
+        nc.sync.dma_start(n1_sb[:], n1)
+        nc.sync.dma_start(n2_sb[:], n2)
+        nc.sync.dma_start(n3_sb[:], n3)
+        nc.sync.dma_start(n4_sb[:], n4)
+        nc.sync.dma_start(out=gain[:], in_=gn.rearrange("(p t) o -> p (t o)", t=PACK))
+        load_scale_rows(nc.sync, w2_scale_raw, 0, w2_scales)
+
+        def deal_words(dealt, raw):
+            nc.vector.tensor_copy(
+                out=dealt[:].rearrange("p (t c i) -> p c t i", t=PACK, i=4),
+                in_=raw[:].rearrange("p (c i t) -> p c t i", t=PACK, i=4),
+            )
+
+        def deal_scales(dealt, raw):
+            nc.vector.tensor_copy(
+                out=dealt[:].rearrange("p (t m) -> p m t", t=PACK),
+                in_=raw[:].rearrange("p (m t) -> p m t", t=PACK),
+            )
+
+        x_scale = sb.tile([P, S], U8, align_bytes=64)
+        x_code = [sb.tile([P, hi - lo], U32, name="x_code%d" % lo, align_bytes=64) for lo, hi in HALVES]
+        w1_code = sb.tile([P, H], I32, align_bytes=64)
+        w1_scale = sb.tile([P, H], U8, align_bytes=64)
+        w2_code = sb.tile([P, N], I32, align_bytes=64)
+        w2_scale = sb.tile([P, N], U8, align_bytes=64)
+
+        deal_words(w1_code, w1_raw)
+        w2_raw = sb.tile([P, N], I32, align_bytes=64, tag="w_raw")
+        nc.sync.dma_start(out=w2_raw[:], in_=as_words(w2_words))
+        nc.vector.tensor_copy(x_scale[:], x_scale_table[:].indirect(offs_sb[:]))
+        nc.vector.tensor_copy(x_code[0][:], x_word_table[:].indirect(entries(offs_sb, *HALVES[0])))
+        deal_scales(w1_scale, w1_scale_raw)
+        nc.vector.tensor_copy(x_code[1][:], x_word_table[:].indirect(entries(offs_sb, *HALVES[1])))
+        deal_words(w2_code, w2_raw)
+        deal_scales(w2_scale, w2_scale_raw)
+
+        y_ps = [ps.tile([P, S], F32, name="y_ps%d" % t, tag="low%d" % t) for t in range(PACK)]
+        for half, (lo, hi) in enumerate(HALVES):
+            for t in range(PACK):
+                cols = slice(t * P, (t + 1) * P)
+                nc.tensor.matmul_mx(
+                    out=y_ps[t][:, lo:hi],
+                    lhsT=w1_code[:, cols].bitcast(FP8X4),
+                    lhsT_scale=w1_scale[:, cols],
+                    rhs=x_code[half][:].bitcast(FP8X4),
+                    rhs_scale=x_scale[:, lo:hi],
+                    start=True,
+                    stop=True,
+                )
+
+        y_plain = sb.tile([P, PACK, S], F32)
+        y_gain = sb.tile([P, PACK, S], F32)
+        st = [sb.tile([P, S], F32, name="st%d" % t) for t in range(PACK)]
+        for t in range(PACK):
+            nc.scalar.copy(y_window[t][:, :S], y_ps[t][:])
+            nc.scalar.copy(y_plain[:, t, :], y_ps[t][:])
+        for t in range(PACK):
+            nc.vector.tensor_tensor(st[t][:], y_window[t][:].indirect(n1_sb[:]), y_plain[:, t, :], ALU.subtract)
+        for t in range(PACK):
+            nc.vector.tensor_scalar_mul(y_gain[:, t, :], y_plain[:, t, :], gain[:, t : t + 1])
+
+        h_first = [ps.tile([P, CHUNKS[-1][0]], F32, name="h_first%d" % t, tag="high%d" % t) for t in range(PACK)]
+        h_last = [ps.tile([P, S - CHUNKS[-1][0]], F32, name="h_last%d" % t, tag="low%d" % t) for t in range(PACK)]
+        for lo, hi in CHUNKS:
+            n = hi - lo
+            gate = sb.tile([P, PACK, n], F32, name="gate%d" % lo)
+            for t in range(PACK):
+                nc.scalar.activation(gate[:, t, :], st[t][:].indirect(entries(n2_sb, lo, hi)), ACT.Sigmoid)
+            z = sb.tile([P, PACK * n], BF16, name="z%d" % lo, align_bytes=64)
+            nc.vector.tensor_tensor(woven(z[:]), by_pairs(y_gain[:, :, lo:hi]), by_pairs(gate[:]), ALU.mult)
+            z_code = sb.tile([P, n], U32, name="z_code%d" % lo, align_bytes=64)
+            z_scale = sb.tile([P, n], U8, name="z_scale%d" % lo, align_bytes=64)
+            nc.vector.quantize_mx(out=z_code[:].bitcast(FP8X4), scales=z_scale[:], in_=z[:])
+            for t in range(PACK):
+                cols = slice(t * P, (t + 1) * P)
+                nc.tensor.matmul_mx(
+                    out=h_last[t][:] if hi == S else h_first[t][:, lo:hi],
+                    lhsT=w2_code[:, cols].bitcast(FP8X4),
+                    lhsT_scale=w2_scale[:, cols],
+                    rhs=z_code[:].bitcast(FP8X4),
+                    rhs_scale=z_scale[:],
+                    start=True,
+                    stop=True,
+                )
+
+        h_neg = [sb.tile([P, S], F32, name="h_neg%d" % t) for t in range(PACK)]
+        h_plain = sb.tile([P, PACK, S], F32)
+        cut = CHUNKS[-1][0]
+        for t in range(PACK):
+            nc.scalar.activation(h_neg[t][:, :cut], h_first[t][:], ACT.Copy, scale=-1.0)
+            nc.scalar.copy(h_plain[:, t, :cut], h_first[t][:])
+            nc.scalar.activation(h_neg[t][:, cut:], h_last[t][:], ACT.Copy, scale=-1.0)
+            nc.scalar.copy(h_plain[:, t, cut:], h_last[t][:])
+
+        out_rows = out_0.rearrange("(p t) c -> p t c", t=PACK)
+        out_words = as_words(out_1)
+        o_scale = sb.tile([P, S], U8, align_bytes=64)
+        for lo, hi in CHUNKS:
+            n = hi - lo
+            less3 = sb.tile([P, PACK, n], F32, name="less3_%d" % lo)
+            less4 = sb.tile([P, PACK, n], F32, name="less4_%d" % lo)
+            for t in range(PACK):
+                nc.vector.tensor_tensor(less3[:, t, :], h_neg[t][:].indirect(entries(n3_sb, lo, hi)), h_plain[:, t, lo:hi], ALU.add)
+                nc.vector.tensor_tensor(less4[:, t, :], h_neg[t][:].indirect(entries(n4_sb, lo, hi)), h_plain[:, t, lo:hi], ALU.add)
+            result = sb.tile([P, PACK, n], F32, name="result%d" % lo)
+            nc.vector.tensor_tensor(result[:], less3[:], less4[:], ALU.max)
+            nc.sync.dma_start(out=out_rows[:, :, lo:hi], in_=result[:])
+            rounded = sb.tile([P, PACK * n], BF16, name="rounded%d" % lo, align_bytes=64)
+            nc.scalar.copy(woven(rounded[:]), by_pairs(result[:]))
+            o_code = sb.tile([P, n], U32, name="o_code%d" % lo, align_bytes=64)
+            nc.vector.quantize_mx(out=o_code[:].bitcast(FP8X4), scales=o_scale[:, lo:hi], in_=rounded[:])
+            nc.sync.dma_start(out=out_words[:, lo:hi], in_=o_code[:].bitcast(I32))
+        for q in range(4):
+            queue = nc.scalar if q % 2 else nc.sync
+            queue.dma_start(out=out_2[0][4 * q : 4 * q + 4, :].bitcast(I32), in_=o_scale[32 * q : 32 * q + 4, :].bitcast(I32))

@@ -16,27 +16,32 @@ ALU = mybir.AluOpType
 ACT = mybir.ActivationFunctionType
 
 P = 128
-PACK = 4
+PLANES = 4
+LAST_PLANE = PLANES - 1
 LIST_ROWS = 16
-W2_ROW = 4
-HALVES = [(0, 256), (256, 512)]
-CHUNKS = [(0, 256), (256, 384), (384, 512)]
+QUADRANTS = 4
+WINDOW = 2 * S
+
+HALVES = [(0, S // 2), (S // 2, S)]
+CHUNKS = [(0, S // 2), (S // 2, 3 * S // 4), (3 * S // 4, S)]
+MIDDLE_START = CHUNKS[1][0]
+LAST_START = CHUNKS[2][0]
 
 
 def as_words(dram):
     return dram[0].rearrange("p n t -> p (n t)").bitcast(I32)
 
 
-def entries(lst, lo, hi):
-    return lst[:, lo // LIST_ROWS : hi // LIST_ROWS]
+def entries(offsets, lo, hi):
+    return offsets[:, lo // LIST_ROWS : hi // LIST_ROWS]
 
 
-def load_scale_rows(queue, plane, first_row, dram):
-    for q in range(4):
-        queue.dma_start(
-            out=plane[32 * q + first_row : 32 * q + first_row + 4, :].bitcast(I32),
-            in_=dram[0][4 * q : 4 * q + 4, :].bitcast(I32),
-        )
+def scale_rows(tile, q):
+    return tile[32 * q : 32 * q + 4, :].bitcast(I32)
+
+
+def dram_scale_rows(dram, q):
+    return dram[0][4 * q : 4 * q + 4, :].bitcast(I32)
 
 
 def by_pairs(planes):
@@ -44,158 +49,185 @@ def by_pairs(planes):
 
 
 def woven(tile):
-    return tile.rearrange("p (c i t) -> p c t i", i=2, t=PACK)
+    return tile.rearrange("p (c i t) -> p c t i", i=2, t=PLANES)
 
 
 def tile_picked_layhopdunder_none_po_kernel(
     tc, x_words, x_scales, w1_words, w1_scales, gn, w2_words, w2_scales, offs, n1, n2, n3, n4, out_0, out_1, out_2
 ):
     nc = tc.nc
+
+    def load_scales(queue, tile, dram):
+        for q in range(QUADRANTS):
+            queue.dma_start(out=scale_rows(tile, q), in_=dram_scale_rows(dram, q))
+
+    def deal_words(dealt, raw):
+        nc.vector.tensor_copy(
+            out=dealt[:].rearrange("p (t c i) -> p c t i", t=PLANES, i=4),
+            in_=raw[:].rearrange("p (c i t) -> p c t i", t=PLANES, i=4),
+        )
+
+    def deal_scales(dealt, raw, t0, t1):
+        nc.vector.tensor_copy(
+            out=dealt.rearrange("p (t m) -> p t m", t=t1 - t0),
+            in_=raw[:].rearrange("p (m t) -> p t m", t=PLANES)[:, t0:t1, :],
+        )
+
+    def product(out, w_code, w_scale, code, scale):
+        nc.tensor.matmul_mx(
+            out=out,
+            lhsT=w_code.bitcast(FP8X4),
+            lhsT_scale=w_scale,
+            rhs=code.bitcast(FP8X4),
+            rhs_scale=scale,
+            start=True,
+            stop=True,
+        )
+
     with ExitStack() as ctx:
         lists = ctx.enter_context(tc.tile_pool(name="lists", bufs=1))
         sb = ctx.enter_context(tc.tile_pool(name="sb", bufs=1))
         ps = ctx.enter_context(tc.psum_pool(name="ps", bufs=1))
 
+
         x_scale_table = sb.tile([P, T], U8, align_bytes=64)
         w1_scale_raw = sb.tile([P, H], U8, align_bytes=64)
-        w2_scale_raw = sb.tile([P, N], U8, align_bytes=64)
-        y_window = [sb.tile([P, 2 * S], F32, name="y_window%d" % t) for t in range(PACK)]
-        warm = sb.tile([P, 1], F32)
+        window = [sb.tile([P, WINDOW], F32, name="window", tag="window%d" % t, align_bytes=64) for t in range(PLANES)]
+        warm_in = sb.tile([P, 1], F32)
         warm_out = sb.tile([P, 1], F32)
-        nc.gpsimd.memset(warm[:], 0.0)
+        nc.gpsimd.memset(w1_scale_raw[:].bitcast(I32), 0)
+        nc.gpsimd.memset(warm_in[:], 0.0)
         nc.vector.memset(x_scale_table[:].bitcast(I32), 0)
-        for t in range(PACK):
-            nc.vector.memset(y_window[t][:, S:], 0.0)
-        nc.vector.memset(w1_scale_raw[:].bitcast(I32), 0)
-        nc.vector.memset(w2_scale_raw[:].bitcast(I32), 0)
+        for t in range(PLANES):
+            nc.vector.memset(window[t][:, S:], 0.0)
 
         offs_sb = lists.tile([P, S // LIST_ROWS], U16)
         n1_sb = lists.tile([P, S // LIST_ROWS], U16)
         n2_sb = lists.tile([P, S // LIST_ROWS], U16)
         n3_sb = lists.tile([P, S // LIST_ROWS], U16)
         n4_sb = lists.tile([P, S // LIST_ROWS], U16)
-        x_word_table = sb.tile([P, T], U32, align_bytes=64)
-        w1_raw = sb.tile([P, H], I32, align_bytes=64, tag="w_raw")
-        gain = sb.tile([P, PACK], F32)
+        x_word_table = sb.tile([P, T], U32, align_bytes=64, tag="x_word_table")
+        w1_raw = sb.tile([P, H], I32, align_bytes=64)
+        w2_raw = sb.tile([P, N], I32, align_bytes=64)
+        gain = sb.tile([P, PLANES], F32)
 
         nc.sync.dma_start(offs_sb[:], offs)
-        nc.scalar.dma_start(out=w1_raw[:], in_=as_words(w1_words))
-        nc.scalar.dma_start(out=x_word_table[:].bitcast(I32), in_=as_words(x_words))
-        load_scale_rows(nc.sync, x_scale_table, 0, x_scales)
-        nc.scalar.activation(warm_out[:], warm[:], ACT.Sigmoid)
-        load_scale_rows(nc.scalar, w1_scale_raw, 0, w1_scales)
+        nc.scalar.dma_start(out=x_word_table[:, : T // 2].bitcast(I32), in_=as_words(x_words)[:, : T // 2])
+        load_scales(nc.sync, x_scale_table, x_scales)
         nc.sync.dma_start(n1_sb[:], n1)
+        nc.sync.dma_start(out=x_word_table[:, T // 2 :].bitcast(I32), in_=as_words(x_words)[:, T // 2 :])
+        nc.sync.dma_start(out=w1_raw[:], in_=as_words(w1_words))
+        load_scales(nc.sync, w1_scale_raw, w1_scales)
+        nc.scalar.activation(warm_out[:], warm_in[:], ACT.Sigmoid)
+        nc.sync.dma_start(out=w2_raw[:], in_=as_words(w2_words))
+        nc.sync.dma_start(out=gain[:], in_=gn.rearrange("(p t) o -> p (t o)", t=PLANES))
         nc.sync.dma_start(n2_sb[:], n2)
         nc.sync.dma_start(n3_sb[:], n3)
         nc.sync.dma_start(n4_sb[:], n4)
-        nc.sync.dma_start(out=gain[:], in_=gn.rearrange("(p t) o -> p (t o)", t=PACK))
-        load_scale_rows(nc.sync, w2_scale_raw, 0, w2_scales)
-
-        def deal_words(dealt, raw):
-            nc.vector.tensor_copy(
-                out=dealt[:].rearrange("p (t c i) -> p c t i", t=PACK, i=4),
-                in_=raw[:].rearrange("p (c i t) -> p c t i", t=PACK, i=4),
-            )
-
-        def deal_scales(dealt, raw):
-            nc.vector.tensor_copy(
-                out=dealt[:].rearrange("p (t m) -> p m t", t=PACK),
-                in_=raw[:].rearrange("p (m t) -> p m t", t=PACK),
-            )
 
         x_scale = sb.tile([P, S], U8, align_bytes=64)
-        x_code = [sb.tile([P, hi - lo], U32, name="x_code%d" % lo, align_bytes=64) for lo, hi in HALVES]
+        x_code = sb.tile([P, S], U32, align_bytes=64)
         w1_code = sb.tile([P, H], I32, align_bytes=64)
         w1_scale = sb.tile([P, H], U8, align_bytes=64)
         w2_code = sb.tile([P, N], I32, align_bytes=64)
-        w2_scale = sb.tile([P, N], U8, align_bytes=64)
-
-        deal_words(w1_code, w1_raw)
-        w2_raw = sb.tile([P, N], I32, align_bytes=64, tag="w_raw")
-        nc.sync.dma_start(out=w2_raw[:], in_=as_words(w2_words))
         nc.vector.tensor_copy(x_scale[:], x_scale_table[:].indirect(offs_sb[:]))
-        nc.vector.tensor_copy(x_code[0][:], x_word_table[:].indirect(entries(offs_sb, *HALVES[0])))
-        deal_scales(w1_scale, w1_scale_raw)
-        nc.vector.tensor_copy(x_code[1][:], x_word_table[:].indirect(entries(offs_sb, *HALVES[1])))
+        nc.vector.tensor_copy(x_code[:], x_word_table[:].indirect(offs_sb[:]))
+        deal_words(w1_code, w1_raw)
+        deal_scales(w1_scale[:, :P], w1_scale_raw, 0, 1)
+        deal_scales(w1_scale[:, P:], w1_scale_raw, 1, PLANES)
         deal_words(w2_code, w2_raw)
-        deal_scales(w2_scale, w2_scale_raw)
 
-        y_ps = [ps.tile([P, S], F32, name="y_ps%d" % t, tag="low%d" % t) for t in range(PACK)]
-        for half, (lo, hi) in enumerate(HALVES):
-            for t in range(PACK):
-                cols = slice(t * P, (t + 1) * P)
-                nc.tensor.matmul_mx(
-                    out=y_ps[t][:, lo:hi],
-                    lhsT=w1_code[:, cols].bitcast(FP8X4),
-                    lhsT_scale=w1_scale[:, cols],
-                    rhs=x_code[half][:].bitcast(FP8X4),
-                    rhs_scale=x_scale[:, lo:hi],
-                    start=True,
-                    stop=True,
-                )
+        w2_scale_raw = sb.tile([P, N], U8, align_bytes=64, tag="x_word_table")
+        nc.gpsimd.memset(w2_scale_raw[:].bitcast(I32), 0)
+        load_scales(nc.scalar, w2_scale_raw, w2_scales)
+        w2_scale_first = sb.tile([P, P], U8, align_bytes=64)
+        deal_scales(w2_scale_first[:], w2_scale_raw, 0, 1)
 
-        y_plain = sb.tile([P, PACK, S], F32)
-        y_gain = sb.tile([P, PACK, S], F32)
-        st = [sb.tile([P, S], F32, name="st%d" % t) for t in range(PACK)]
-        for t in range(PACK):
-            nc.scalar.copy(y_window[t][:, :S], y_ps[t][:])
-            nc.scalar.copy(y_plain[:, t, :], y_ps[t][:])
-        for t in range(PACK):
-            nc.vector.tensor_tensor(st[t][:], y_window[t][:].indirect(n1_sb[:]), y_plain[:, t, :], ALU.subtract)
-        for t in range(PACK):
+        y_plain = sb.tile([P, PLANES, S], F32)
+        st = [sb.tile([P, S], F32, name="st%d" % t) for t in range(PLANES)]
+        for t in range(PLANES):
+            cols = slice(t * P, (t + 1) * P)
+            for part, (lo, hi) in enumerate(HALVES if t == 0 else [(0, S)]):
+                y_ps = ps.tile([P, hi - lo], F32, name="y_ps", tag="bank%d_%d" % (part, t))
+                product(y_ps[:], w1_code[:, cols], w1_scale[:, cols], x_code[:, lo:hi], x_scale[:, lo:hi])
+                nc.scalar.copy(window[t][:, lo:hi], y_ps[:])
+                if t == 0:
+                    nc.vector.tensor_copy(y_plain[:, t, lo:hi], y_ps[:])
+                else:
+                    nc.scalar.copy(y_plain[:, t, lo:hi], y_ps[:])
+        for t in range(PLANES):
+            nc.vector.tensor_tensor(st[t][:], window[t][:].indirect(n1_sb[:]), y_plain[:, t, :], ALU.subtract)
+
+        y_gain = sb.tile([P, PLANES, S], F32, tag="window%d" % LAST_PLANE, align_bytes=64)
+        for t in range(PLANES):
             nc.vector.tensor_scalar_mul(y_gain[:, t, :], y_plain[:, t, :], gain[:, t : t + 1])
 
-        h_first = [ps.tile([P, CHUNKS[-1][0]], F32, name="h_first%d" % t, tag="high%d" % t) for t in range(PACK)]
-        h_last = [ps.tile([P, S - CHUNKS[-1][0]], F32, name="h_last%d" % t, tag="low%d" % t) for t in range(PACK)]
+        h_chunk = {lo: ps.tile([P, hi - lo], F32, name="h_chunk", tag="bank1_%d" % c) for c, (lo, hi) in enumerate(CHUNKS)}
+        z_scale = sb.tile([P, S], U8, align_bytes=64)
+        z = {}
         for lo, hi in CHUNKS:
-            n = hi - lo
-            gate = sb.tile([P, PACK, n], F32, name="gate%d" % lo)
-            for t in range(PACK):
+            gate = sb.tile([P, PLANES, hi - lo], F32, name="gate", tag="gate%d" % lo, align_bytes=64)
+            for t in range(PLANES):
                 nc.scalar.activation(gate[:, t, :], st[t][:].indirect(entries(n2_sb, lo, hi)), ACT.Sigmoid)
-            z = sb.tile([P, PACK * n], BF16, name="z%d" % lo, align_bytes=64)
-            nc.vector.tensor_tensor(woven(z[:]), by_pairs(y_gain[:, :, lo:hi]), by_pairs(gate[:]), ALU.mult)
-            z_code = sb.tile([P, n], U32, name="z_code%d" % lo, align_bytes=64)
-            z_scale = sb.tile([P, n], U8, name="z_scale%d" % lo, align_bytes=64)
-            nc.vector.quantize_mx(out=z_code[:].bitcast(FP8X4), scales=z_scale[:], in_=z[:])
-            for t in range(PACK):
-                cols = slice(t * P, (t + 1) * P)
-                nc.tensor.matmul_mx(
-                    out=h_last[t][:] if hi == S else h_first[t][:, lo:hi],
-                    lhsT=w2_code[:, cols].bitcast(FP8X4),
-                    lhsT_scale=w2_scale[:, cols],
-                    rhs=z_code[:].bitcast(FP8X4),
-                    rhs_scale=z_scale[:],
-                    start=True,
-                    stop=True,
-                )
+            z[lo] = sb.tile([P, PLANES * (hi - lo)], BF16, name="z", tag="z%d" % lo, align_bytes=64)
+            nc.vector.tensor_tensor(woven(z[lo][:]), by_pairs(y_gain[:, :, lo:hi]), by_pairs(gate[:]), ALU.mult)
 
-        h_neg = [sb.tile([P, S], F32, name="h_neg%d" % t) for t in range(PACK)]
-        h_plain = sb.tile([P, PACK, S], F32)
-        cut = CHUNKS[-1][0]
-        for t in range(PACK):
-            nc.scalar.activation(h_neg[t][:, :cut], h_first[t][:], ACT.Copy, scale=-1.0)
-            nc.scalar.copy(h_plain[:, t, :cut], h_first[t][:])
-            nc.scalar.activation(h_neg[t][:, cut:], h_last[t][:], ACT.Copy, scale=-1.0)
-            nc.scalar.copy(h_plain[:, t, cut:], h_last[t][:])
-
-        out_rows = out_0.rearrange("(p t) c -> p t c", t=PACK)
-        out_words = as_words(out_1)
-        o_scale = sb.tile([P, S], U8, align_bytes=64)
+        z_code = sb.tile([P, S], U32, tag="gate%d" % MIDDLE_START, align_bytes=64)
         for lo, hi in CHUNKS:
-            n = hi - lo
-            less3 = sb.tile([P, PACK, n], F32, name="less3_%d" % lo)
-            less4 = sb.tile([P, PACK, n], F32, name="less4_%d" % lo)
-            for t in range(PACK):
-                nc.vector.tensor_tensor(less3[:, t, :], h_neg[t][:].indirect(entries(n3_sb, lo, hi)), h_plain[:, t, lo:hi], ALU.add)
-                nc.vector.tensor_tensor(less4[:, t, :], h_neg[t][:].indirect(entries(n4_sb, lo, hi)), h_plain[:, t, lo:hi], ALU.add)
-            result = sb.tile([P, PACK, n], F32, name="result%d" % lo)
-            nc.vector.tensor_tensor(result[:], less3[:], less4[:], ALU.max)
-            nc.sync.dma_start(out=out_rows[:, :, lo:hi], in_=result[:])
-            rounded = sb.tile([P, PACK * n], BF16, name="rounded%d" % lo, align_bytes=64)
-            nc.scalar.copy(woven(rounded[:]), by_pairs(result[:]))
-            o_code = sb.tile([P, n], U32, name="o_code%d" % lo, align_bytes=64)
-            nc.vector.quantize_mx(out=o_code[:].bitcast(FP8X4), scales=o_scale[:, lo:hi], in_=rounded[:])
-            nc.sync.dma_start(out=out_words[:, lo:hi], in_=o_code[:].bitcast(I32))
-        for q in range(4):
-            queue = nc.scalar if q % 2 else nc.sync
-            queue.dma_start(out=out_2[0][4 * q : 4 * q + 4, :].bitcast(I32), in_=o_scale[32 * q : 32 * q + 4, :].bitcast(I32))
+            nc.vector.quantize_mx(out=z_code[:, lo:hi].bitcast(FP8X4), scales=z_scale[:, lo:hi], in_=z[lo][:])
+            product(h_chunk[lo][:], w2_code[:, :P], w2_scale_first[:], z_code[:, lo:hi], z_scale[:, lo:hi])
+
+        last_window = sb.tile([P, S], F32)
+        h_neg = window[:LAST_PLANE] + [last_window]
+        h_plain = sb.tile([P, PLANES, S], F32)
+        w2_scale_rest = sb.tile([P, N - P], U8, tag="z%d" % LAST_START, align_bytes=64)
+        deal_scales(w2_scale_rest[:], w2_scale_raw, 1, PLANES)
+        for lo, hi in CHUNKS[:-1]:
+            nc.scalar.activation(h_neg[0][:, lo:hi], h_chunk[lo][:], ACT.Copy, scale=-1.0)
+            nc.scalar.copy(h_plain[:, 0, lo:hi], h_chunk[lo][:])
+        nc.vector.tensor_scalar_mul(h_neg[0][:, LAST_START:S], h_chunk[LAST_START][:], -1.0)
+        nc.vector.tensor_copy(h_plain[:, 0, LAST_START:], h_chunk[LAST_START][:])
+        for t in range(1, PLANES):
+            h_ps = ps.tile([P, S], F32, name="h_ps", tag="bank0_%d" % t)
+            product(h_ps[:], w2_code[:, t * P : (t + 1) * P], w2_scale_rest[:, (t - 1) * P : t * P], z_code[:], z_scale[:])
+            nc.scalar.activation(h_neg[t][:, :S], h_ps[:], ACT.Copy, scale=-1.0)
+            nc.scalar.copy(h_plain[:, t, :], h_ps[:])
+
+        out_rows = out_0.rearrange("(p t) c -> p t c", t=PLANES)
+        out_words = as_words(out_1)
+        out_scale = sb.tile([P, S], U8, align_bytes=64)
+        less3 = sb.tile([P, PLANES, S], F32)
+        less4 = sb.tile([P, PLANES, S], F32)
+        result = sb.tile([P, PLANES, S], F32)
+
+        def differences(t, lo, hi):
+            for less, offsets in ((less3, n3_sb), (less4, n4_sb)):
+                looked_up = h_neg[t][:].indirect(entries(offsets, lo, hi))
+                nc.vector.tensor_tensor(less[:, t, lo:hi], looked_up, h_plain[:, t, lo:hi], ALU.add)
+
+        def store_larger(t, lo, hi):
+            cells = (slice(None), slice(t, t + 1), slice(lo, hi))
+            nc.vector.tensor_tensor(result[cells], less3[cells], less4[cells], ALU.max)
+            nc.sync.dma_start(out=out_rows[cells], in_=result[cells])
+
+        for t in range(LAST_PLANE):
+            differences(t, 0, S)
+            store_larger(t, 0, S)
+        for lo, hi in CHUNKS:
+            rounded = sb.tile([P, PLANES * (hi - lo)], BF16, name="rounded%d" % lo, align_bytes=64)
+            differences(LAST_PLANE, lo, hi)
+            if lo == LAST_START:
+                nc.vector.tensor_tensor(
+                    woven(rounded[:]), by_pairs(less3[:, :, lo:hi]), by_pairs(less4[:, :, lo:hi]), ALU.max
+                )
+                store_larger(LAST_PLANE, lo, hi)
+            else:
+                store_larger(LAST_PLANE, lo, hi)
+                nc.scalar.copy(woven(rounded[:]), by_pairs(result[:, :, lo:hi]))
+            out_code = sb.tile([P, hi - lo], U32, name="out_code%d" % lo, align_bytes=64)
+            nc.vector.quantize_mx(out=out_code[:].bitcast(FP8X4), scales=out_scale[:, lo:hi], in_=rounded[:])
+            nc.sync.dma_start(out=out_words[:, lo:hi], in_=out_code[:].bitcast(I32))
+
+        for q in range(QUADRANTS):
+            queue = nc.sync if q == QUADRANTS - 1 else nc.scalar
+            queue.dma_start(out=dram_scale_rows(out_2, q), in_=scale_rows(out_scale, q))

from contextlib import ExitStack

import concourse.mybir as mybir

K, T, S, N, H = 512, 2048, 512, 512, 512
FLOPS = 2 * K * H * S + 2 * H * N * S

F32 = mybir.dt.float32
BF16 = mybir.dt.bfloat16
I32 = mybir.dt.int32
U32 = mybir.dt.uint32
U16 = mybir.dt.uint16
U8 = mybir.dt.uint8
FP8X4 = mybir.dt.float8_e4m3fn_x4
ALU = mybir.AluOpType
ACT = mybir.ActivationFunctionType

P = 128
PLANES = 4
LAST_PLANE = PLANES - 1
LIST_ROWS = 16
QUADRANTS = 4
WINDOW = 2 * S

HALVES = [(0, S // 2), (S // 2, S)]
CHUNKS = [(0, S // 2), (S // 2, 3 * S // 4), (3 * S // 4, S)]
MIDDLE_START = CHUNKS[1][0]
LAST_START = CHUNKS[2][0]


def as_words(dram):
    return dram[0].rearrange("p n t -> p (n t)").bitcast(I32)


def entries(offsets, lo, hi):
    return offsets[:, lo // LIST_ROWS : hi // LIST_ROWS]


def scale_rows(tile, q):
    return tile[32 * q : 32 * q + 4, :].bitcast(I32)


def dram_scale_rows(dram, q):
    return dram[0][4 * q : 4 * q + 4, :].bitcast(I32)


def by_pairs(planes):
    return planes.rearrange("p t (c i) -> p c t i", i=2)


def woven(tile):
    return tile.rearrange("p (c i t) -> p c t i", i=2, t=PLANES)


def tile_picked_layhopdunder_none_po_kernel(
    tc, x_words, x_scales, w1_words, w1_scales, gn, w2_words, w2_scales, offs, n1, n2, n3, n4, out_0, out_1, out_2
):
    nc = tc.nc

    def load_scales(queue, tile, dram):
        for q in range(QUADRANTS):
            queue.dma_start(out=scale_rows(tile, q), in_=dram_scale_rows(dram, q))

    def deal_words(dealt, raw):
        nc.vector.tensor_copy(
            out=dealt[:].rearrange("p (t c i) -> p c t i", t=PLANES, i=4),
            in_=raw[:].rearrange("p (c i t) -> p c t i", t=PLANES, i=4),
        )

    def deal_scales(dealt, raw, t0, t1):
        nc.vector.tensor_copy(
            out=dealt.rearrange("p (t m) -> p t m", t=t1 - t0),
            in_=raw[:].rearrange("p (m t) -> p t m", t=PLANES)[:, t0:t1, :],
        )

    def product(out, w_code, w_scale, code, scale):
        nc.tensor.matmul_mx(
            out=out,
            lhsT=w_code.bitcast(FP8X4),
            lhsT_scale=w_scale,
            rhs=code.bitcast(FP8X4),
            rhs_scale=scale,
            start=True,
            stop=True,
        )

    with ExitStack() as ctx:
        lists = ctx.enter_context(tc.tile_pool(name="lists", bufs=1))
        sb = ctx.enter_context(tc.tile_pool(name="sb", bufs=1))
        ps = ctx.enter_context(tc.psum_pool(name="ps", bufs=1))


        x_scale_table = sb.tile([P, T], U8, align_bytes=64)
        w1_scale_raw = sb.tile([P, H], U8, align_bytes=64)
        window = [sb.tile([P, WINDOW], F32, name="window", tag="window%d" % t, align_bytes=64) for t in range(PLANES)]
        warm_in = sb.tile([P, 1], F32)
        warm_out = sb.tile([P, 1], F32)
        nc.gpsimd.memset(w1_scale_raw[:].bitcast(I32), 0)
        nc.gpsimd.memset(warm_in[:], 0.0)
        nc.vector.memset(x_scale_table[:].bitcast(I32), 0)
        for t in range(PLANES):
            nc.vector.memset(window[t][:, S:], 0.0)

        offs_sb = lists.tile([P, S // LIST_ROWS], U16)
        n1_sb = lists.tile([P, S // LIST_ROWS], U16)
        n2_sb = lists.tile([P, S // LIST_ROWS], U16)
        n3_sb = lists.tile([P, S // LIST_ROWS], U16)
        n4_sb = lists.tile([P, S // LIST_ROWS], U16)
        x_word_table = sb.tile([P, T], U32, align_bytes=64, tag="x_word_table")
        w1_raw = sb.tile([P, H], I32, align_bytes=64)
        w2_raw = sb.tile([P, N], I32, align_bytes=64)
        gain = sb.tile([P, PLANES], F32)

        nc.sync.dma_start(offs_sb[:], offs)
        nc.scalar.dma_start(out=x_word_table[:, : T // 2].bitcast(I32), in_=as_words(x_words)[:, : T // 2])
        load_scales(nc.sync, x_scale_table, x_scales)
        nc.sync.dma_start(n1_sb[:], n1)
        nc.sync.dma_start(out=x_word_table[:, T // 2 :].bitcast(I32), in_=as_words(x_words)[:, T // 2 :])
        nc.sync.dma_start(out=w1_raw[:], in_=as_words(w1_words))
        load_scales(nc.sync, w1_scale_raw, w1_scales)
        nc.scalar.activation(warm_out[:], warm_in[:], ACT.Sigmoid)
        nc.sync.dma_start(out=w2_raw[:], in_=as_words(w2_words))
        nc.sync.dma_start(out=gain[:], in_=gn.rearrange("(p t) o -> p (t o)", t=PLANES))
        nc.sync.dma_start(n2_sb[:], n2)
        nc.sync.dma_start(n3_sb[:], n3)
        nc.sync.dma_start(n4_sb[:], n4)

        x_scale = sb.tile([P, S], U8, align_bytes=64)
        x_code = sb.tile([P, S], U32, align_bytes=64)
        w1_code = sb.tile([P, H], I32, align_bytes=64)
        w1_scale = sb.tile([P, H], U8, align_bytes=64)
        w2_code = sb.tile([P, N], I32, align_bytes=64)
        nc.vector.tensor_copy(x_scale[:], x_scale_table[:].indirect(offs_sb[:]))
        nc.vector.tensor_copy(x_code[:], x_word_table[:].indirect(offs_sb[:]))
        deal_words(w1_code, w1_raw)
        deal_scales(w1_scale[:, :P], w1_scale_raw, 0, 1)
        deal_scales(w1_scale[:, P:], w1_scale_raw, 1, PLANES)
        deal_words(w2_code, w2_raw)

        w2_scale_raw = sb.tile([P, N], U8, align_bytes=64, tag="x_word_table")
        nc.gpsimd.memset(w2_scale_raw[:].bitcast(I32), 0)
        load_scales(nc.scalar, w2_scale_raw, w2_scales)
        w2_scale_first = sb.tile([P, P], U8, align_bytes=64)
        deal_scales(w2_scale_first[:], w2_scale_raw, 0, 1)

        y_plain = sb.tile([P, PLANES, S], F32)
        st = [sb.tile([P, S], F32, name="st%d" % t) for t in range(PLANES)]
        for t in range(PLANES):
            cols = slice(t * P, (t + 1) * P)
            for part, (lo, hi) in enumerate(HALVES if t == 0 else [(0, S)]):
                y_ps = ps.tile([P, hi - lo], F32, name="y_ps", tag="bank%d_%d" % (part, t))
                product(y_ps[:], w1_code[:, cols], w1_scale[:, cols], x_code[:, lo:hi], x_scale[:, lo:hi])
                nc.scalar.copy(window[t][:, lo:hi], y_ps[:])
                if t == 0:
                    nc.vector.tensor_copy(y_plain[:, t, lo:hi], y_ps[:])
                else:
                    nc.scalar.copy(y_plain[:, t, lo:hi], y_ps[:])
        for t in range(PLANES):
            nc.vector.tensor_tensor(st[t][:], window[t][:].indirect(n1_sb[:]), y_plain[:, t, :], ALU.subtract)

        y_gain = sb.tile([P, PLANES, S], F32, tag="window%d" % LAST_PLANE, align_bytes=64)
        for t in range(PLANES):
            nc.vector.tensor_scalar_mul(y_gain[:, t, :], y_plain[:, t, :], gain[:, t : t + 1])

        h_chunk = {lo: ps.tile([P, hi - lo], F32, name="h_chunk", tag="bank1_%d" % c) for c, (lo, hi) in enumerate(CHUNKS)}
        z_scale = sb.tile([P, S], U8, align_bytes=64)
        z = {}
        for lo, hi in CHUNKS:
            gate = sb.tile([P, PLANES, hi - lo], F32, name="gate", tag="gate%d" % lo, align_bytes=64)
            for t in range(PLANES):
                nc.scalar.activation(gate[:, t, :], st[t][:].indirect(entries(n2_sb, lo, hi)), ACT.Sigmoid)
            z[lo] = sb.tile([P, PLANES * (hi - lo)], BF16, name="z", tag="z%d" % lo, align_bytes=64)
            nc.vector.tensor_tensor(woven(z[lo][:]), by_pairs(y_gain[:, :, lo:hi]), by_pairs(gate[:]), ALU.mult)

        z_code = sb.tile([P, S], U32, tag="gate%d" % MIDDLE_START, align_bytes=64)
        for lo, hi in CHUNKS:
            nc.vector.quantize_mx(out=z_code[:, lo:hi].bitcast(FP8X4), scales=z_scale[:, lo:hi], in_=z[lo][:])
            product(h_chunk[lo][:], w2_code[:, :P], w2_scale_first[:], z_code[:, lo:hi], z_scale[:, lo:hi])

        last_window = sb.tile([P, S], F32)
        h_neg = window[:LAST_PLANE] + [last_window]
        h_plain = sb.tile([P, PLANES, S], F32)
        w2_scale_rest = sb.tile([P, N - P], U8, tag="z%d" % LAST_START, align_bytes=64)
        deal_scales(w2_scale_rest[:], w2_scale_raw, 1, PLANES)
        for lo, hi in CHUNKS[:-1]:
            nc.scalar.activation(h_neg[0][:, lo:hi], h_chunk[lo][:], ACT.Copy, scale=-1.0)
            nc.scalar.copy(h_plain[:, 0, lo:hi], h_chunk[lo][:])
        nc.vector.tensor_scalar_mul(h_neg[0][:, LAST_START:S], h_chunk[LAST_START][:], -1.0)
        nc.vector.tensor_copy(h_plain[:, 0, LAST_START:], h_chunk[LAST_START][:])
        for t in range(1, PLANES):
            h_ps = ps.tile([P, S], F32, name="h_ps", tag="bank0_%d" % t)
            product(h_ps[:], w2_code[:, t * P : (t + 1) * P], w2_scale_rest[:, (t - 1) * P : t * P], z_code[:], z_scale[:])
            nc.scalar.activation(h_neg[t][:, :S], h_ps[:], ACT.Copy, scale=-1.0)
            nc.scalar.copy(h_plain[:, t, :], h_ps[:])

        out_rows = out_0.rearrange("(p t) c -> p t c", t=PLANES)
        out_words = as_words(out_1)
        out_scale = sb.tile([P, S], U8, align_bytes=64)
        less3 = sb.tile([P, PLANES, S], F32)
        less4 = sb.tile([P, PLANES, S], F32)
        result = sb.tile([P, PLANES, S], F32)

        def differences(t, lo, hi):
            for less, offsets in ((less3, n3_sb), (less4, n4_sb)):
                looked_up = h_neg[t][:].indirect(entries(offsets, lo, hi))
                nc.vector.tensor_tensor(less[:, t, lo:hi], looked_up, h_plain[:, t, lo:hi], ALU.add)

        def store_larger(t, lo, hi):
            cells = (slice(None), slice(t, t + 1), slice(lo, hi))
            nc.vector.tensor_tensor(result[cells], less3[cells], less4[cells], ALU.max)
            nc.sync.dma_start(out=out_rows[cells], in_=result[cells])

        for t in range(LAST_PLANE):
            differences(t, 0, S)
            store_larger(t, 0, S)
        for lo, hi in CHUNKS:
            rounded = sb.tile([P, PLANES * (hi - lo)], BF16, name="rounded%d" % lo, align_bytes=64)
            differences(LAST_PLANE, lo, hi)
            if lo == LAST_START:
                nc.vector.tensor_tensor(
                    woven(rounded[:]), by_pairs(less3[:, :, lo:hi]), by_pairs(less4[:, :, lo:hi]), ALU.max
                )
                store_larger(LAST_PLANE, lo, hi)
            else:
                store_larger(LAST_PLANE, lo, hi)
                nc.scalar.copy(woven(rounded[:]), by_pairs(result[:, :, lo:hi]))
            out_code = sb.tile([P, hi - lo], U32, name="out_code%d" % lo, align_bytes=64)
            nc.vector.quantize_mx(out=out_code[:].bitcast(FP8X4), scales=out_scale[:, lo:hi], in_=rounded[:])
            nc.sync.dma_start(out=out_words[:, lo:hi], in_=out_code[:].bitcast(I32))

        for q in range(QUADRANTS):
            queue = nc.sync if q == QUADRANTS - 1 else nc.scalar
            queue.dma_start(out=dram_scale_rows(out_2, q), in_=scale_rows(out_scale, q))
